import numpy as np
import ml_dtypes


def mxq(x, axis, fmt="e4m3"):
    dtype, down = {"e4m3": (ml_dtypes.float8_e4m3fn, 7), "e5m2": (ml_dtypes.float8_e5m2, 14)}[fmt]
    v = np.moveaxis(np.asarray(x, np.float32).astype(ml_dtypes.bfloat16).astype(np.float64), axis, -1)
    blocks = v.reshape(v.shape[:-1] + (-1, 32))
    amax = np.abs(blocks).max(-1, keepdims=True)
    byte = np.maximum(np.where(amax > 0, np.frexp(amax)[1] - 1 + 127, 0) - down, 1)
    scale = np.exp2(byte - 127.0)
    codes = (blocks / scale).astype(np.float32).astype(dtype).astype(np.float64)
    return np.moveaxis((codes * scale).reshape(v.shape), -1, axis)


WIDE = False


def mx_kscale(k):
    if not WIDE:
        return np.ones(k)
    levels = np.array([10, -10, 5, -5, 0])
    if k % 512:
        return np.exp2(np.random.permutation(np.resize(levels, k // 32))).repeat(32)
    a = np.empty((k // 512, 16))
    for p in range(k // 512):
        a[p, :8] = np.random.permutation(np.resize(levels, 8))
        for g in range(8):
            far = levels[np.abs(levels - a[p, g]) >= 10]
            a[p, g + 8] = far[np.random.randint(len(far))]
    return np.exp2(a.ravel()).repeat(32)


def f64(x):
    return np.asarray(x).astype(np.float64)


def striped(idx):
    return np.tile(idx.reshape(-1, 16).T, (8, 1)).astype(np.uint16)


def unstriped(offs):
    return offs[:16].T.reshape(-1).astype(np.int64)


E2M1 = np.array([0.0, 0.5, 1.0, 1.5, 2.0, 3.0, 4.0, 6.0, -0.0, -0.5, -1.0, -1.5, -2.0, -3.0, -4.0, -6.0])


def pack_weight(w, fmt):
    k, n = w.shape
    w = f64(np.asarray(w, np.float32).astype(ml_dtypes.bfloat16)).reshape(k // 32, 32, n)
    amax = np.abs(w).max(1)
    if fmt == "e4m3":
        byte = np.frexp(amax)[1] - 1 + 127 - 7
    else:
        mant, ex = np.frexp(amax / 6.0)
        byte = np.where(mant > 0.5, ex, ex - 1) + 127
    byte = np.clip(np.where(amax > 0, byte, 1), 1, 254)
    scaled = (w * np.exp2(127.0 - byte)[:, None, :]).reshape(k, n).astype(np.float32)
    by_word = np.ascontiguousarray(scaled.reshape(k // 512, 128, 4, n).transpose(0, 1, 3, 2))
    if fmt == "e4m3":
        words = by_word.astype(ml_dtypes.float8_e4m3fn).view(np.uint8)
    else:
        c = by_word.astype(ml_dtypes.float4_e2m1fn).view(np.uint8) & 0xF
        words = (c[..., 0::2] | (c[..., 1::2] << 4)).reshape(k // 512, 128, 2 * n)
    return np.ascontiguousarray(words), np.ascontiguousarray(byte.astype(np.uint8).reshape(k // 512, 16, n))


def unpack_weight(words, scales, fmt):
    g, _, n = scales.shape
    words = np.ascontiguousarray(words).reshape(g, 128, n, -1)
    if fmt == "e4m3":
        vals = words.view(ml_dtypes.float8_e4m3fn).astype(np.float64)
    else:
        nib = np.empty((g, 128, n, 4), np.uint8)
        nib[..., 0::2] = words & 0xF
        nib[..., 1::2] = words >> 4
        vals = E2M1[nib]
    vals = vals * np.repeat(np.exp2(scales.astype(np.float64) - 127.0), 8, axis=1)[..., None]
    return vals.transpose(0, 1, 3, 2).reshape(g * 512, n)


def gelu(v):
    return 0.5 * v * (1.0 + np.tanh(np.sqrt(2.0 / np.pi) * (v + 0.044715 * v**3)))


K, T, E, C, H, N = 512, 384, 12, 128, 512, 256
TOP = 4


def by_expert(wq, xq):
    return np.concatenate([wq[e].T @ xq[:, e * C:(e + 1) * C] for e in range(E)], axis=1)


def setup_inputs():
    n = np.random.standard_normal
    s = mx_kscale(K)[:, None]
    u = mx_kscale(H)
    deal = np.repeat(np.arange(E), C).reshape(TOP, T)[:, np.random.permutation(T)]
    deal = np.take_along_axis(deal, np.argsort(np.random.rand(TOP, T), axis=0), axis=0)
    for _ in range(8):
        s_, t_ = np.random.permutation(T).reshape(2, -1); r = np.random.randint(TOP, size=T // 2); x, y = deal[r, s_].copy(), deal[r, t_].copy()
        ok = ~((deal[:, s_] == y).any(0) | (deal[:, t_] == x).any(0)); deal[r[ok], s_[ok]] = y[ok]; deal[r[ok], t_[ok]] = x[ok]
    order = np.lexsort((np.random.rand(TOP * T), deal.reshape(-1)))
    slot_token = order % T; pos = np.empty(TOP * T, np.int64); pos[order] = np.arange(TOP * T); pos = pos.reshape(TOP, T)
    g = np.random.uniform(0.5, 1.5, (TOP, T)); g = g / g.sum(0)
    w1 = [pack_weight(m, "e2m1") for m in n((E, K, H)) / np.sqrt(K) / s[None]]
    w3 = [pack_weight(m, "e2m1") for m in n((E, K, H)) / np.sqrt(K) / s[None] * u[None, None, :]]
    w2 = [pack_weight(m, "e2m1") for m in n((E, H, N)) / np.sqrt(H) / u[None, :, None]]
    return {
        "xT": (n((K, T)) * s).astype(np.float32),
        "w1_words": np.stack([m[0] for m in w1]),
        "w1_scales": np.stack([m[1] for m in w1]),
        "w3_words": np.stack([m[0] for m in w3]),
        "w3_scales": np.stack([m[1] for m in w3]),
        "w2_words": np.stack([m[0] for m in w2]),
        "w2_scales": np.stack([m[1] for m in w2]),
        "gate": np.stack([np.tile(r, (N, 1)) for r in g]).astype(np.float32),
        "offs": striped(slot_token),
        "pos1": striped(pos[0]),
        "pos2": striped(pos[1]),
        "pos3": striped(pos[2]),
        "pos4": striped(pos[3]),
    }


def reference(xT, w1_words, w1_scales, w3_words, w3_scales, w2_words, w2_scales, gate, offs, pos1, pos2, pos3, pos4):
    idx = unstriped(offs)
    w1 = np.stack([unpack_weight(w1_words[e], w1_scales[e], "e2m1") for e in range(E)])
    w3 = np.stack([unpack_weight(w3_words[e], w3_scales[e], "e2m1") for e in range(E)])
    w2 = np.stack([unpack_weight(w2_words[e], w2_scales[e], "e2m1") for e in range(E)])
    xq = mxq(f64(xT)[:, idx], 0, "e4m3")
    h = gelu(by_expert(w1, xq))
    h = h * by_expert(w3, xq)
    y = by_expert(w2, mxq(h, 0, "e4m3"))
    return sum(f64(gate[r]) * y[:, unstriped(p)] for r, p in enumerate((pos1, pos2, pos3, pos4)))

@@ -1,0 +1,281 @@
+from contextlib import ExitStack
+
+import concourse.mybir as mybir
+from concourse.masks import make_identity
+
+K, T, E, C, H, N = 512, 384, 12, 128, 512, 256
+TOP = 4
+S = E * C
+P = 128
+HALVES = N // P
+WINDOW = 512
+
+FLOPS = 2 * S * (2 * K * H + H * N)
+
+F32 = mybir.dt.float32
+BF16 = mybir.dt.bfloat16
+I32 = mybir.dt.int32
+U32 = mybir.dt.uint32
+U16 = mybir.dt.uint16
+U8 = mybir.dt.uint8
+FP8X4 = mybir.dt.float8_e4m3fn_x4
+FP4X4 = mybir.dt.float4_e2m1fn_x4
+GELU = mybir.ActivationFunctionType.Gelu_apprx_tanh
+ADD, MULT = mybir.AluOpType.add, mybir.AluOpType.mult
+
+GATHER_GROUPS = [(0, 1), (1, 2), (2, 4), (4, 6), (6, 8), (8, 10), (10, 12)]
+SCALE_GROUPS = [(0, 3), (3, 12)]
+X_CHUNKS = [(0, 256, 160), (256, 384, 80)]
+
+
+def tile_moe_tk_glu_gelu_kernel(
+    tc, xT, w1_words, w1_scales, w3_words, w3_scales, w2_words, w2_scales, gate, offs, pos1, pos2, pos3, pos4, out
+):
+    nc = tc.nc
+    with ExitStack() as ctx:
+        lists = ctx.enter_context(tc.tile_pool(name="lists", bufs=1))
+        keep = ctx.enter_context(tc.tile_pool(name="keep", bufs=1))
+        ring = ctx.enter_context(tc.tile_pool(name="ring", bufs=3))
+        psum = ctx.enter_context(tc.psum_pool(name="psum", bufs=2))
+
+        offs_t = lists.tile([P, S // 16], U16, name="offs_t")
+        pos_t = [lists.tile([P, T // 16], U16, name=f"pos_t{r}") for r in range(TOP)]
+
+        s1 = keep.tile([P, E, H], U8, name="s1", align_bytes=64)
+        s3 = keep.tile([P, E, H], U8, name="s3", align_bytes=64)
+        s2 = keep.tile([P, E, N], U8, name="s2", align_bytes=64)
+        w1 = keep.tile([P, E, 2 * H], U8, name="w1", align_bytes=64)
+        w3 = keep.tile([P, E, 2 * H], U8, name="w3", align_bytes=64)
+        w2 = keep.tile([P, E, 2 * N], U8, name="w2", align_bytes=64)
+        gate_t = keep.tile([P, TOP, HALVES, T], F32, name="gate_t", align_bytes=64)
+        codes = keep.tile([P, WINDOW], I32, name="codes", align_bytes=64)
+        cscale = keep.tile([P, WINDOW], U8, name="cscale", align_bytes=64)
+        ident = keep.tile([P, P], F32, name="ident", align_bytes=64)
+        warm = keep.tile([P, 1], F32, name="warm")
+        y = [keep.tile([P, S], F32, name=f"y{h}", align_bytes=64) for h in range(HALVES)]
+        prod = keep.tile([P, TOP, HALVES, T], F32, name="prod", align_bytes=64)
+
+        nc.vector.memset(warm[:], 0.0)
+        for a, b in SCALE_GROUPS:
+            nc.vector.memset(s1[:, a:b, :].bitcast(I32), 0)
+            nc.vector.memset(s3[:, a:b, :].bitcast(I32), 0)
+        nc.vector.memset(s2[:].bitcast(I32), 0)
+        nc.vector.memset(codes[:, T:WINDOW], 0)
+        nc.gpsimd.memset(cscale[:], 0)
+        warm_out = keep.tile([P, 1], F32, name="warm_out")
+        nc.scalar.activation(warm_out[:], warm[:], GELU)
+
+        make_identity(nc, ident[:])
+
+        x_rows = xT.rearrange("(p j) w -> p j w", j=4)
+        raw = []
+        for i, (a, b, split) in enumerate(X_CHUNKS):
+            chunk = keep.tile([P, 4, b - a], F32, name=f"raw{i}", align_bytes=64)
+            nc.sync.dma_start(out=chunk[:], in_=x_rows[:, :, a:b])
+            raw.append(chunk)
+        nc.sync.dma_start(offs_t[:], offs)
+
+        def load_words(tile, words, a, b):
+            nc.sync.dma_start(
+                out=tile[:, a:b, :].bitcast(I32),
+                in_=words[a:b, 0, :, :].rearrange("e p n -> p e n").bitcast(I32),
+            )
+
+        def load_scales(queue, tile, scales, a, b):
+            for q in range(4):
+                queue.dma_start(
+                    out=tile[32 * q : 32 * q + 4, a:b, :].bitcast(I32),
+                    in_=scales[a:b, 0, 4 * q : 4 * q + 4, :].rearrange("e q n -> q e n").bitcast(I32),
+                )
+
+        load_words(w1, w1_words, 0, 1)
+        load_words(w3, w3_words, 0, 1)
+        load_scales(nc.sync, s1, w1_scales, 0, 3)
+        load_scales(nc.sync, s3, w3_scales, 0, 3)
+        load_scales(nc.gpsimd, s1, w1_scales, 3, E)
+        load_scales(nc.gpsimd, s3, w3_scales, 3, E)
+        load_scales(nc.sync, s2, w2_scales, 0, 3)
+        load_words(w1, w1_words, 1, 2)
+        load_words(w3, w3_words, 1, 2)
+        load_words(w2, w2_words, 0, 2)
+        load_words(w1, w1_words, 2, 4)
+        load_words(w3, w3_words, 2, 4)
+        load_scales(nc.sync, s2, w2_scales, 3, E)
+        load_words(w2, w2_words, 2, 4)
+        for a in range(4, E, 2):
+            load_words(w1, w1_words, a, a + 2)
+            load_words(w3, w3_words, a, a + 2)
+            load_words(w2, w2_words, a, a + 2)
+        for r, pos in enumerate((pos1, pos2, pos3, pos4)):
+            nc.sync.dma_start(pos_t[r][:], pos)
+        for r in range(TOP):
+            nc.sync.dma_start(out=gate_t[:, r, :, :], in_=gate[r].rearrange("(h p) t -> p h t", p=P))
+
+        for i, (a, b, split) in enumerate(X_CHUNKS):
+            grouped = keep.tile([P, b - a, 4], BF16, name=f"grouped{i}", align_bytes=64)
+            turned = raw[i][:].rearrange("p j w -> p w j")
+            nc.vector.tensor_copy(out=grouped[:, :split, :], in_=turned[:, :split, :])
+            nc.scalar.copy(out=grouped[:, split:, :], in_=turned[:, split:, :])
+            nc.vector.quantize_mx(
+                out=codes[:, a:b].bitcast(FP8X4),
+                scales=cscale[:, a:b],
+                in_=grouped[:].rearrange("p w j -> p (w j)"),
+            )
+
+        slot_words = {}
+        slot_scales = {}
+        live = {}
+
+        def gather(g):
+            a, b = GATHER_GROUPS[g]
+            width = (b - a) * C
+            where = offs_t[:, a * C // 16 : b * C // 16]
+            gs = keep.tile([P, width], U8, name=f"gs{g}", align_bytes=64)
+            nc.vector.tensor_copy(gs[:], cscale[:].indirect(where))
+            gw = keep.tile([P, width], U32, name=f"gw{g}", align_bytes=64)
+            nc.vector.tensor_copy(gw[:], codes[:].bitcast(U32).indirect(where))
+            for e in range(a, b):
+                cols = slice((e - a) * C, (e - a + 1) * C)
+                slot_words[e] = gw[:, cols]
+                slot_scales[e] = gs[:, cols]
+
+        def first_layer(e):
+            pa = psum.tile([P, H], F32, name="pa")
+            pb = psum.tile([P, H], F32, name="pb")
+            for bank, words, scales in ((pa, w1, s1), (pb, w3, s3)):
+                nc.tensor.matmul_mx(
+                    out=bank[:],
+                    lhsT=slot_words[e].bitcast(FP8X4),
+                    lhsT_scale=slot_scales[e],
+                    rhs=words[:, e, :].bitcast(FP4X4),
+                    rhs_scale=scales[:, e, :],
+                    start=True,
+                    stop=True,
+                )
+            live[e] = (pa, pb)
+
+        def activate(e):
+            pa, pb = live[e]
+            g = ring.tile([P, H], F32, name="g", align_bytes=64)
+            nc.scalar.activation(
+                out=g[:].rearrange("p (u m e) -> p u m e", u=2, e=2),
+                in_=pa[:].rearrange("p (m u e) -> p u m e", u=2, e=2),
+                func=GELU,
+            )
+            live[e] = (g, pb)
+
+        def multiply(e):
+            g, pb = live[e]
+            h = ring.tile([P, H], BF16, name="h", align_bytes=64)
+            nc.vector.tensor_tensor(
+                out=h[:].rearrange("p (u m e) -> p u m e", u=2, e=2),
+                in0=pb[:].rearrange("p (m u e) -> p u m e", u=2, e=2),
+                in1=g[:].rearrange("p (u m e) -> p u m e", u=2, e=2),
+                op=MULT,
+            )
+            live[e] = h
+
+        def turn(e):
+            h = live[e]
+            pt = psum.tile([P, 2, C], F32, name="pt")
+            words = h[:].bitcast(F32)
+            for u in range(2):
+                nc.tensor.transpose(pt[:, u, :], words[:, u * P : (u + 1) * P], ident[:])
+            live[e] = pt
+
+        def turn_out(e):
+            pt = live[e]
+            ht = ring.tile([P, 4 * C], BF16, name="ht", align_bytes=64)
+            nc.scalar.copy(
+                out=ht[:].bitcast(F32).rearrange("p (s u) -> p s u", u=2),
+                in_=pt[:].rearrange("p u s -> p s u"),
+            )
+            live[e] = ht
+
+        def quantise(e):
+            ht = live[e]
+            hw = ring.tile([P, C], U32, name="hw", align_bytes=64)
+            hs = ring.tile([P, C], U8, name="hs", align_bytes=64)
+            nc.vector.quantize_mx(out=hw[:].bitcast(FP8X4), scales=hs[:], in_=ht[:])
+            live[e] = (hw, hs)
+
+        banks = {}
+
+        def second_layer(e):
+            hw, hs = live[e]
+            if e % 2 == 0:
+                banks[e // 2] = psum.tile([P, HALVES, 2, C], F32, name="py")
+            py = banks[e // 2]
+            for half in range(HALVES):
+                nc.tensor.matmul_mx(
+                    out=py[:, half, e % 2, :],
+                    lhsT=w2[:, e, 2 * P * half : 2 * P * (half + 1)].bitcast(FP4X4),
+                    lhsT_scale=s2[:, e, P * half : P * (half + 1)],
+                    rhs=hw[:].bitcast(FP8X4),
+                    rhs_scale=hs[:],
+                    start=True,
+                    stop=True,
+                )
+
+        def results(e):
+            py = banks[e // 2]
+            if e >= E - 2:
+                nc.scalar.copy(out=y[0][:, e * C : (e + 1) * C], in_=py[:, 0, e % 2, :])
+                nc.vector.tensor_copy(out=y[1][:, e * C : (e + 1) * C], in_=py[:, 1, e % 2, :])
+            elif e % 2 == 1:
+                for half in range(HALVES):
+                    nc.scalar.copy(
+                        out=y[half][:, (e - 1) * C : (e + 1) * C].rearrange("p (b c) -> p b c", b=2),
+                        in_=py[:, half, :, :],
+                    )
+
+        group_of = {}
+        for g, (a, b) in enumerate(GATHER_GROUPS):
+            group_of[a] = g
+
+        gather(0)
+        first_layer(0)
+        for step in range(E + 2):
+            if step < E:
+                activate(step)
+            if step + 1 < E:
+                if step + 1 in group_of:
+                    gather(group_of[step + 1])
+                first_layer(step + 1)
+            if 0 <= step - 1 < E:
+                turn_out(step - 1)
+            if step < E:
+                multiply(step)
+                turn(step)
+            if 0 <= step - 1 < E:
+                quantise(step - 1)
+                second_layer(step - 1)
+                results(step - 1)
+
+        def fetch(r, half):
+            nc.vector.tensor_tensor(prod[:, r, half, :], y[half][:].indirect(pos_t[r][:]), gate_t[:, r, half, :], MULT)
+
+        def add(half, to, left, right):
+            nc.vector.tensor_tensor(to, left, right, ADD)
+
+        sums = keep.tile([P, HALVES, 3, T], F32, name="sums", align_bytes=64)
+
+        def store(half):
+            nc.sync.dma_start(out=out[half * P : (half + 1) * P, :], in_=sums[:, half, 2, :])
+
+        fetch(0, 0)
+        fetch(1, 0)
+        fetch(2, 0)
+        add(0, sums[:, 0, 0, :], prod[:, 0, 0, :], prod[:, 1, 0, :])
+        fetch(3, 0)
+        add(0, sums[:, 0, 1, :], sums[:, 0, 0, :], prod[:, 2, 0, :])
+        fetch(0, 1)
+        add(0, sums[:, 0, 2, :], sums[:, 0, 1, :], prod[:, 3, 0, :])
+        store(0)
+        fetch(1, 1)
+        fetch(2, 1)
+        add(1, sums[:, 1, 0, :], prod[:, 0, 1, :], prod[:, 1, 1, :])
+        fetch(3, 1)
+        add(1, sums[:, 1, 1, :], sums[:, 1, 0, :], prod[:, 2, 1, :])
+        add(1, sums[:, 1, 2, :], sums[:, 1, 1, :], prod[:, 3, 1, :])
+        store(1)

@@ -24,7 +24,7 @@ GELU = mybir.ActivationFunctionType.Gelu_apprx_tanh
 ADD, MULT = mybir.AluOpType.add, mybir.AluOpType.mult
 
 GATHER_GROUPS = [(0, 1), (1, 2), (2, 4), (4, 6), (6, 8), (8, 10), (10, 12)]
-SCALE_GROUPS = [(0, 3), (3, 12)]
+WORD_GROUPS = [(2, 4), (4, 6), (6, 9), (9, 12)]
 X_CHUNKS = [(0, 256, 160), (256, 384, 80)]
 
 
@@ -36,6 +36,7 @@ def tile_moe_tk_glu_gelu_kernel(
         lists = ctx.enter_context(tc.tile_pool(name="lists", bufs=1))
         keep = ctx.enter_context(tc.tile_pool(name="keep", bufs=1))
         ring = ctx.enter_context(tc.tile_pool(name="ring", bufs=3))
+        pair = ctx.enter_context(tc.tile_pool(name="pair", bufs=3))
         psum = ctx.enter_context(tc.psum_pool(name="psum", bufs=2))
 
         offs_t = lists.tile([P, S // 16], U16, name="offs_t")
@@ -56,16 +57,24 @@ def tile_moe_tk_glu_gelu_kernel(
         prod = keep.tile([P, TOP, HALVES, T], F32, name="prod", align_bytes=64)
 
         nc.vector.memset(warm[:], 0.0)
-        for a, b in SCALE_GROUPS:
-            nc.vector.memset(s1[:, a:b, :].bitcast(I32), 0)
-            nc.vector.memset(s3[:, a:b, :].bitcast(I32), 0)
-        nc.vector.memset(s2[:].bitcast(I32), 0)
         nc.vector.memset(codes[:, T:WINDOW], 0)
         nc.gpsimd.memset(cscale[:], 0)
+        make_identity(nc, ident[:])
         warm_out = keep.tile([P, 1], F32, name="warm_out")
         nc.scalar.activation(warm_out[:], warm[:], GELU)
 
-        make_identity(nc, ident[:])
+        def load_words(tile, words, a, b):
+            nc.sync.dma_start(
+                out=tile[:, a:b, :].bitcast(I32),
+                in_=words[a:b, 0, :, :].rearrange("e p n -> p e n").bitcast(I32),
+            )
+
+        def load_scales(tile, scales):
+            for q in range(4):
+                nc.sync.dma_start(
+                    out=tile[32 * q : 32 * q + 4, :, :].bitcast(I32),
+                    in_=scales[:, 0, 4 * q : 4 * q + 4, :].rearrange("e q n -> q e n").bitcast(I32),
+                )
 
         x_rows = xT.rearrange("(p j) w -> p j w", j=4)
         raw = []
@@ -74,42 +83,24 @@ def tile_moe_tk_glu_gelu_kernel(
             nc.sync.dma_start(out=chunk[:], in_=x_rows[:, :, a:b])
             raw.append(chunk)
         nc.sync.dma_start(offs_t[:], offs)
-
-        def load_words(tile, words, a, b):
-            nc.sync.dma_start(
-                out=tile[:, a:b, :].bitcast(I32),
-                in_=words[a:b, 0, :, :].rearrange("e p n -> p e n").bitcast(I32),
-            )
-
-        def load_scales(queue, tile, scales, a, b):
-            for q in range(4):
-                queue.dma_start(
-                    out=tile[32 * q : 32 * q + 4, a:b, :].bitcast(I32),
-                    in_=scales[a:b, 0, 4 * q : 4 * q + 4, :].rearrange("e q n -> q e n").bitcast(I32),
-                )
-
+        load_scales(s1, w1_scales)
         load_words(w1, w1_words, 0, 1)
+        load_scales(s3, w3_scales)
         load_words(w3, w3_words, 0, 1)
-        load_scales(nc.sync, s1, w1_scales, 0, 3)
-        load_scales(nc.sync, s3, w3_scales, 0, 3)
-        load_scales(nc.gpsimd, s1, w1_scales, 3, E)
-        load_scales(nc.gpsimd, s3, w3_scales, 3, E)
-        load_scales(nc.sync, s2, w2_scales, 0, 3)
         load_words(w1, w1_words, 1, 2)
         load_words(w3, w3_words, 1, 2)
         load_words(w2, w2_words, 0, 2)
-        load_words(w1, w1_words, 2, 4)
-        load_words(w3, w3_words, 2, 4)
-        load_scales(nc.sync, s2, w2_scales, 3, E)
-        load_words(w2, w2_words, 2, 4)
-        for a in range(4, E, 2):
-            load_words(w1, w1_words, a, a + 2)
-            load_words(w3, w3_words, a, a + 2)
-            load_words(w2, w2_words, a, a + 2)
+        load_scales(s2, w2_scales)
+        for a, b in WORD_GROUPS:
+            load_words(w1, w1_words, a, b)
+            load_words(w3, w3_words, a, b)
+            load_words(w2, w2_words, a, b)
         for r, pos in enumerate((pos1, pos2, pos3, pos4)):
             nc.sync.dma_start(pos_t[r][:], pos)
-        for r in range(TOP):
-            nc.sync.dma_start(out=gate_t[:, r, :, :], in_=gate[r].rearrange("(h p) t -> p h t", p=P))
+        nc.sync.dma_start(
+            out=gate_t[:].rearrange("p r h t -> p (r h) t"),
+            in_=gate.rearrange("r n t -> (r n) t").rearrange("(g p) t -> p g t", p=P),
+        )
 
         for i, (a, b, split) in enumerate(X_CHUNKS):
             grouped = keep.tile([P, b - a, 4], BF16, name=f"grouped{i}", align_bytes=64)
@@ -130,9 +121,9 @@ def tile_moe_tk_glu_gelu_kernel(
             a, b = GATHER_GROUPS[g]
             width = (b - a) * C
             where = offs_t[:, a * C // 16 : b * C // 16]
-            gs = keep.tile([P, width], U8, name=f"gs{g}", align_bytes=64)
+            gs = pair.tile([P, width], U8, name="gs", align_bytes=64)
             nc.vector.tensor_copy(gs[:], cscale[:].indirect(where))
-            gw = keep.tile([P, width], U32, name=f"gw{g}", align_bytes=64)
+            gw = pair.tile([P, width], U32, name="gw", align_bytes=64)
             nc.vector.tensor_copy(gw[:], codes[:].bitcast(U32).indirect(where))
             for e in range(a, b):
                 cols = slice((e - a) * C, (e - a + 1) * C)

from contextlib import ExitStack

import concourse.mybir as mybir
from concourse.masks import make_identity

K, T, E, C, H, N = 512, 384, 12, 128, 512, 256
TOP = 4
S = E * C
P = 128
HALVES = N // P
WINDOW = 512

FLOPS = 2 * S * (2 * K * H + H * N)

F32 = mybir.dt.float32
BF16 = mybir.dt.bfloat16
I32 = mybir.dt.int32
U32 = mybir.dt.uint32
U16 = mybir.dt.uint16
U8 = mybir.dt.uint8
FP8X4 = mybir.dt.float8_e4m3fn_x4
FP4X4 = mybir.dt.float4_e2m1fn_x4
GELU = mybir.ActivationFunctionType.Gelu_apprx_tanh
ADD, MULT = mybir.AluOpType.add, mybir.AluOpType.mult

GATHER_GROUPS = [(0, 1), (1, 2), (2, 4), (4, 6), (6, 8), (8, 10), (10, 12)]
WORD_GROUPS = [(2, 4), (4, 6), (6, 9), (9, 12)]
X_CHUNKS = [(0, 256, 160), (256, 384, 80)]


def tile_moe_tk_glu_gelu_kernel(
    tc, xT, w1_words, w1_scales, w3_words, w3_scales, w2_words, w2_scales, gate, offs, pos1, pos2, pos3, pos4, out
):
    nc = tc.nc
    with ExitStack() as ctx:
        lists = ctx.enter_context(tc.tile_pool(name="lists", bufs=1))
        keep = ctx.enter_context(tc.tile_pool(name="keep", bufs=1))
        ring = ctx.enter_context(tc.tile_pool(name="ring", bufs=3))
        pair = ctx.enter_context(tc.tile_pool(name="pair", bufs=3))
        psum = ctx.enter_context(tc.psum_pool(name="psum", bufs=2))

        offs_t = lists.tile([P, S // 16], U16, name="offs_t")
        pos_t = [lists.tile([P, T // 16], U16, name=f"pos_t{r}") for r in range(TOP)]

        s1 = keep.tile([P, E, H], U8, name="s1", align_bytes=64)
        s3 = keep.tile([P, E, H], U8, name="s3", align_bytes=64)
        s2 = keep.tile([P, E, N], U8, name="s2", align_bytes=64)
        w1 = keep.tile([P, E, 2 * H], U8, name="w1", align_bytes=64)
        w3 = keep.tile([P, E, 2 * H], U8, name="w3", align_bytes=64)
        w2 = keep.tile([P, E, 2 * N], U8, name="w2", align_bytes=64)
        gate_t = keep.tile([P, TOP, HALVES, T], F32, name="gate_t", align_bytes=64)
        codes = keep.tile([P, WINDOW], I32, name="codes", align_bytes=64)
        cscale = keep.tile([P, WINDOW], U8, name="cscale", align_bytes=64)
        ident = keep.tile([P, P], F32, name="ident", align_bytes=64)
        warm = keep.tile([P, 1], F32, name="warm")
        y = [keep.tile([P, S], F32, name=f"y{h}", align_bytes=64) for h in range(HALVES)]
        prod = keep.tile([P, TOP, HALVES, T], F32, name="prod", align_bytes=64)

        nc.vector.memset(warm[:], 0.0)
        nc.vector.memset(codes[:, T:WINDOW], 0)
        nc.gpsimd.memset(cscale[:], 0)
        make_identity(nc, ident[:])
        warm_out = keep.tile([P, 1], F32, name="warm_out")
        nc.scalar.activation(warm_out[:], warm[:], GELU)

        def load_words(tile, words, a, b):
            nc.sync.dma_start(
                out=tile[:, a:b, :].bitcast(I32),
                in_=words[a:b, 0, :, :].rearrange("e p n -> p e n").bitcast(I32),
            )

        def load_scales(tile, scales):
            for q in range(4):
                nc.sync.dma_start(
                    out=tile[32 * q : 32 * q + 4, :, :].bitcast(I32),
                    in_=scales[:, 0, 4 * q : 4 * q + 4, :].rearrange("e q n -> q e n").bitcast(I32),
                )

        x_rows = xT.rearrange("(p j) w -> p j w", j=4)
        raw = []
        for i, (a, b, split) in enumerate(X_CHUNKS):
            chunk = keep.tile([P, 4, b - a], F32, name=f"raw{i}", align_bytes=64)
            nc.sync.dma_start(out=chunk[:], in_=x_rows[:, :, a:b])
            raw.append(chunk)
        nc.sync.dma_start(offs_t[:], offs)
        load_scales(s1, w1_scales)
        load_words(w1, w1_words, 0, 1)
        load_scales(s3, w3_scales)
        load_words(w3, w3_words, 0, 1)
        load_words(w1, w1_words, 1, 2)
        load_words(w3, w3_words, 1, 2)
        load_words(w2, w2_words, 0, 2)
        load_scales(s2, w2_scales)
        for a, b in WORD_GROUPS:
            load_words(w1, w1_words, a, b)
            load_words(w3, w3_words, a, b)
            load_words(w2, w2_words, a, b)
        for r, pos in enumerate((pos1, pos2, pos3, pos4)):
            nc.sync.dma_start(pos_t[r][:], pos)
        nc.sync.dma_start(
            out=gate_t[:].rearrange("p r h t -> p (r h) t"),
            in_=gate.rearrange("r n t -> (r n) t").rearrange("(g p) t -> p g t", p=P),
        )

        for i, (a, b, split) in enumerate(X_CHUNKS):
            grouped = keep.tile([P, b - a, 4], BF16, name=f"grouped{i}", align_bytes=64)
            turned = raw[i][:].rearrange("p j w -> p w j")
            nc.vector.tensor_copy(out=grouped[:, :split, :], in_=turned[:, :split, :])
            nc.scalar.copy(out=grouped[:, split:, :], in_=turned[:, split:, :])
            nc.vector.quantize_mx(
                out=codes[:, a:b].bitcast(FP8X4),
                scales=cscale[:, a:b],
                in_=grouped[:].rearrange("p w j -> p (w j)"),
            )

        slot_words = {}
        slot_scales = {}
        live = {}

        def gather(g):
            a, b = GATHER_GROUPS[g]
            width = (b - a) * C
            where = offs_t[:, a * C // 16 : b * C // 16]
            gs = pair.tile([P, width], U8, name="gs", align_bytes=64)
            nc.vector.tensor_copy(gs[:], cscale[:].indirect(where))
            gw = pair.tile([P, width], U32, name="gw", align_bytes=64)
            nc.vector.tensor_copy(gw[:], codes[:].bitcast(U32).indirect(where))
            for e in range(a, b):
                cols = slice((e - a) * C, (e - a + 1) * C)
                slot_words[e] = gw[:, cols]
                slot_scales[e] = gs[:, cols]

        def first_layer(e):
            pa = psum.tile([P, H], F32, name="pa")
            pb = psum.tile([P, H], F32, name="pb")
            for bank, words, scales in ((pa, w1, s1), (pb, w3, s3)):
                nc.tensor.matmul_mx(
                    out=bank[:],
                    lhsT=slot_words[e].bitcast(FP8X4),
                    lhsT_scale=slot_scales[e],
                    rhs=words[:, e, :].bitcast(FP4X4),
                    rhs_scale=scales[:, e, :],
                    start=True,
                    stop=True,
                )
            live[e] = (pa, pb)

        def activate(e):
            pa, pb = live[e]
            g = ring.tile([P, H], F32, name="g", align_bytes=64)
            nc.scalar.activation(
                out=g[:].rearrange("p (u m e) -> p u m e", u=2, e=2),
                in_=pa[:].rearrange("p (m u e) -> p u m e", u=2, e=2),
                func=GELU,
            )
            live[e] = (g, pb)

        def multiply(e):
            g, pb = live[e]
            h = ring.tile([P, H], BF16, name="h", align_bytes=64)
            nc.vector.tensor_tensor(
                out=h[:].rearrange("p (u m e) -> p u m e", u=2, e=2),
                in0=pb[:].rearrange("p (m u e) -> p u m e", u=2, e=2),
                in1=g[:].rearrange("p (u m e) -> p u m e", u=2, e=2),
                op=MULT,
            )
            live[e] = h

        def turn(e):
            h = live[e]
            pt = psum.tile([P, 2, C], F32, name="pt")
            words = h[:].bitcast(F32)
            for u in range(2):
                nc.tensor.transpose(pt[:, u, :], words[:, u * P : (u + 1) * P], ident[:])
            live[e] = pt

        def turn_out(e):
            pt = live[e]
            ht = ring.tile([P, 4 * C], BF16, name="ht", align_bytes=64)
            nc.scalar.copy(
                out=ht[:].bitcast(F32).rearrange("p (s u) -> p s u", u=2),
                in_=pt[:].rearrange("p u s -> p s u"),
            )
            live[e] = ht

        def quantise(e):
            ht = live[e]
            hw = ring.tile([P, C], U32, name="hw", align_bytes=64)
            hs = ring.tile([P, C], U8, name="hs", align_bytes=64)
            nc.vector.quantize_mx(out=hw[:].bitcast(FP8X4), scales=hs[:], in_=ht[:])
            live[e] = (hw, hs)

        banks = {}

        def second_layer(e):
            hw, hs = live[e]
            if e % 2 == 0:
                banks[e // 2] = psum.tile([P, HALVES, 2, C], F32, name="py")
            py = banks[e // 2]
            for half in range(HALVES):
                nc.tensor.matmul_mx(
                    out=py[:, half, e % 2, :],
                    lhsT=w2[:, e, 2 * P * half : 2 * P * (half + 1)].bitcast(FP4X4),
                    lhsT_scale=s2[:, e, P * half : P * (half + 1)],
                    rhs=hw[:].bitcast(FP8X4),
                    rhs_scale=hs[:],
                    start=True,
                    stop=True,
                )

        def results(e):
            py = banks[e // 2]
            if e >= E - 2:
                nc.scalar.copy(out=y[0][:, e * C : (e + 1) * C], in_=py[:, 0, e % 2, :])
                nc.vector.tensor_copy(out=y[1][:, e * C : (e + 1) * C], in_=py[:, 1, e % 2, :])
            elif e % 2 == 1:
                for half in range(HALVES):
                    nc.scalar.copy(
                        out=y[half][:, (e - 1) * C : (e + 1) * C].rearrange("p (b c) -> p b c", b=2),
                        in_=py[:, half, :, :],
                    )

        group_of = {}
        for g, (a, b) in enumerate(GATHER_GROUPS):
            group_of[a] = g

        gather(0)
        first_layer(0)
        for step in range(E + 2):
            if step < E:
                activate(step)
            if step + 1 < E:
                if step + 1 in group_of:
                    gather(group_of[step + 1])
                first_layer(step + 1)
            if 0 <= step - 1 < E:
                turn_out(step - 1)
            if step < E:
                multiply(step)
                turn(step)
            if 0 <= step - 1 < E:
                quantise(step - 1)
                second_layer(step - 1)
                results(step - 1)

        def fetch(r, half):
            nc.vector.tensor_tensor(prod[:, r, half, :], y[half][:].indirect(pos_t[r][:]), gate_t[:, r, half, :], MULT)

        def add(half, to, left, right):
            nc.vector.tensor_tensor(to, left, right, ADD)

        sums = keep.tile([P, HALVES, 3, T], F32, name="sums", align_bytes=64)

        def store(half):
            nc.sync.dma_start(out=out[half * P : (half + 1) * P, :], in_=sums[:, half, 2, :])

        fetch(0, 0)
        fetch(1, 0)
        fetch(2, 0)
        add(0, sums[:, 0, 0, :], prod[:, 0, 0, :], prod[:, 1, 0, :])
        fetch(3, 0)
        add(0, sums[:, 0, 1, :], sums[:, 0, 0, :], prod[:, 2, 0, :])
        fetch(0, 1)
        add(0, sums[:, 0, 2, :], sums[:, 0, 1, :], prod[:, 3, 0, :])
        store(0)
        fetch(1, 1)
        fetch(2, 1)
        add(1, sums[:, 1, 0, :], prod[:, 0, 1, :], prod[:, 1, 1, :])
        fetch(3, 1)
        add(1, sums[:, 1, 1, :], sums[:, 1, 0, :], prod[:, 2, 1, :])
        add(1, sums[:, 1, 2, :], sums[:, 1, 1, :], prod[:, 3, 1, :])
        store(1)
